import numpy as np
import ml_dtypes


def mxq(x, axis, fmt="e4m3"):
    dtype, down = {"e4m3": (ml_dtypes.float8_e4m3fn, 7), "e5m2": (ml_dtypes.float8_e5m2, 14)}[fmt]
    v = np.moveaxis(np.asarray(x, np.float32).astype(ml_dtypes.bfloat16).astype(np.float64), axis, -1)
    blocks = v.reshape(v.shape[:-1] + (-1, 32))
    amax = np.abs(blocks).max(-1, keepdims=True)
    byte = np.maximum(np.where(amax > 0, np.frexp(amax)[1] - 1 + 127, 0) - down, 1)
    scale = np.exp2(byte - 127.0)
    codes = (blocks / scale).astype(np.float32).astype(dtype).astype(np.float64)
    return np.moveaxis((codes * scale).reshape(v.shape), -1, axis)


WIDE = False


def mx_kscale(k):
    if not WIDE:
        return np.ones(k)
    levels = np.array([10, -10, 5, -5, 0])
    if k % 512:
        return np.exp2(np.random.permutation(np.resize(levels, k // 32))).repeat(32)
    a = np.empty((k // 512, 16))
    for p in range(k // 512):
        a[p, :8] = np.random.permutation(np.resize(levels, 8))
        for g in range(8):
            far = levels[np.abs(levels - a[p, g]) >= 10]
            a[p, g + 8] = far[np.random.randint(len(far))]
    return np.exp2(a.ravel()).repeat(32)


def f64(x):
    return np.asarray(x).astype(np.float64)


def striped(idx):
    return np.tile(idx.reshape(-1, 16).T, (8, 1)).astype(np.uint16)


def unstriped(offs):
    return offs[:16].T.reshape(-1).astype(np.int64)


E2M1 = np.array([0.0, 0.5, 1.0, 1.5, 2.0, 3.0, 4.0, 6.0, -0.0, -0.5, -1.0, -1.5, -2.0, -3.0, -4.0, -6.0])


def pack_weight(w, fmt):
    k, n = w.shape
    w = f64(np.asarray(w, np.float32).astype(ml_dtypes.bfloat16)).reshape(k // 32, 32, n)
    amax = np.abs(w).max(1)
    if fmt == "e4m3":
        byte = np.frexp(amax)[1] - 1 + 127 - 7
    else:
        mant, ex = np.frexp(amax / 6.0)
        byte = np.where(mant > 0.5, ex, ex - 1) + 127
    byte = np.clip(np.where(amax > 0, byte, 1), 1, 254)
    scaled = (w * np.exp2(127.0 - byte)[:, None, :]).reshape(k, n).astype(np.float32)
    by_word = np.ascontiguousarray(scaled.reshape(k // 512, 128, 4, n).transpose(0, 1, 3, 2))
    if fmt == "e4m3":
        words = by_word.astype(ml_dtypes.float8_e4m3fn).view(np.uint8)
    else:
        c = by_word.astype(ml_dtypes.float4_e2m1fn).view(np.uint8) & 0xF
        words = (c[..., 0::2] | (c[..., 1::2] << 4)).reshape(k // 512, 128, 2 * n)
    return np.ascontiguousarray(words), np.ascontiguousarray(byte.astype(np.uint8).reshape(k // 512, 16, n))


def unpack_weight(words, scales, fmt):
    g, _, n = scales.shape
    words = np.ascontiguousarray(words).reshape(g, 128, n, -1)
    if fmt == "e4m3":
        vals = words.view(ml_dtypes.float8_e4m3fn).astype(np.float64)
    else:
        nib = np.empty((g, 128, n, 4), np.uint8)
        nib[..., 0::2] = words & 0xF
        nib[..., 1::2] = words >> 4
        vals = E2M1[nib]
    vals = vals * np.repeat(np.exp2(scales.astype(np.float64) - 127.0), 8, axis=1)[..., None]
    return vals.transpose(0, 1, 3, 2).reshape(g * 512, n)


def gelu(v):
    return 0.5 * v * (1.0 + np.tanh(np.sqrt(2.0 / np.pi) * (v + 0.044715 * v**3)))


def often(T, S):
    return np.random.permutation(T)[(T * np.random.uniform(0, 1, S) ** 4).astype(np.int64)]


K, K2, H, N, T, S, P = 1024, 512, 1024, 384, 2048, 1024, 512

def setup_inputs():
    n = np.random.standard_normal
    s = mx_kscale(K)[:, None]
    s2 = mx_kscale(K2)[:, None]
    u = mx_kscale(H)[:, None]
    d = {}
    d["tab_words"], d["tab_scales"] = pack_weight(n((K, T)) * s, "e4m3")
    d["tab2_words"], d["tab2_scales"] = pack_weight(n((K2, T)) * s2, "e4m3")
    d["tab3_words"], d["tab3_scales"] = pack_weight(n((K2, T)) * s2, "e4m3")
    d["offs"] = striped(np.random.permutation(T)[:S])
    d["offs2"] = striped(np.random.permutation(T)[:S])
    d["offs3"] = striped(np.random.permutation(T)[:S])
    d["pos1"] = striped(np.random.permutation(S)[:P])
    d["pos2"] = striped(often(S, P))
    d["pos3"] = striped(often(S, P))
    d["w1"] = (n((K, H)) / K**0.5 / s * u.T).astype(np.float32)
    d["w2_words"], d["w2_scales"] = pack_weight(1.2 * n((K2, H)) / K2**0.5 / s2, "e2m1")
    d["b0"] = (0.5 * n(H)).astype(np.float32)
    d["w3_words"], d["w3_scales"] = pack_weight(n((K2, H)) / K2**0.5 / s2 * u.T, "e4m3")
    d["w4"] = (n((H, N)) / H**0.5 / u).astype(np.float32)
    d["w5_words"], d["w5_scales"] = pack_weight(0.6 * n((H, N)) / H**0.5 / u, "e2m1")
    return d

def reference(tab_words, tab_scales, tab2_words, tab2_scales, tab3_words, tab3_scales, offs, offs2, offs3,
              pos1, pos2, pos3, w1, w2_words, w2_scales, b0, w3_words, w3_scales, w4, w5_words, w5_scales):
    v = unpack_weight(tab_words, tab_scales, "e4m3")[:, unstriped(offs)]
    v2 = unpack_weight(tab2_words, tab2_scales, "e4m3")[:, unstriped(offs2)]
    v3 = unpack_weight(tab3_words, tab3_scales, "e4m3")[:, unstriped(offs3)]
    a = mxq(f64(w1), 0, "e4m3").T @ v
    b = unpack_weight(w2_words, w2_scales, "e2m1").T @ v2
    d = unpack_weight(w3_words, w3_scales, "e4m3").T @ v3
    gain = np.exp(np.tanh(b[:, unstriped(pos2)] + f64(b0)[:, None]))
    z = a[:, unstriped(pos1)] * gain + d[:, unstriped(pos3)]
    zq = mxq(z, 0, "e4m3")
    y1 = mxq(f64(w4), 0, "e4m3").T @ zq
    y2 = unpack_weight(w5_words, w5_scales, "e2m1").T @ zq
    return y1 - np.square(y2)

@@ -1,0 +1,267 @@
+from contextlib import ExitStack
+
+import concourse.mybir as mybir
+
+K, K2, H, N, T, S, PICKS = 1024, 512, 1024, 384, 2048, 1024, 512
+FLOPS = 2 * S * H * (K + 2 * K2) + 2 * 2 * H * N * PICKS
+
+F32 = mybir.dt.float32
+BF16 = mybir.dt.bfloat16
+I32 = mybir.dt.int32
+U32 = mybir.dt.uint32
+U16 = mybir.dt.uint16
+U8 = mybir.dt.uint8
+FP8X4 = mybir.dt.float8_e4m3fn_x4
+FP4X4 = mybir.dt.float4_e2m1fn_x4
+ACT = mybir.ActivationFunctionType
+ALU = mybir.AluOpType
+
+P = 128
+PACK = 4
+PASS = P * PACK
+BANK = 512
+
+
+def tile_list_roast_profile_join_kernel(
+    tc, tab_words, tab_scales, tab2_words, tab2_scales, tab3_words, tab3_scales, offs, offs2, offs3,
+    pos1, pos2, pos3, w1, w2_words, w2_scales, b0, w3_words, w3_scales, w4, w5_words, w5_scales, out,
+):
+    nc = tc.nc
+    with ExitStack() as ctx:
+        lists = ctx.enter_context(tc.tile_pool(name="lists", bufs=1))
+        keep = ctx.enter_context(tc.tile_pool(name="keep", bufs=1))
+        loads = ctx.enter_context(tc.tile_pool(name="loads", bufs=1))
+        rounded = ctx.enter_context(tc.tile_pool(name="rounded", bufs=2))
+        windows = ctx.enter_context(tc.tile_pool(name="windows", bufs=14))
+        picks = ctx.enter_context(tc.tile_pool(name="picks", bufs=3))
+        gains = ctx.enter_context(tc.tile_pool(name="gains", bufs=6))
+        joined = ctx.enter_context(tc.tile_pool(name="joined", bufs=2))
+        psum = ctx.enter_context(tc.psum_pool(name="psum", bufs=8))
+
+        def load_list(src, name):
+            tile = lists.tile(list(src.shape), U16, name=name)
+            nc.sync.dma_start(tile[:], src)
+            return tile
+
+        def load_table_words(words, name, slot):
+            tile = loads.tile([P, T], U32, name=name, tag=slot, align_bytes=64)
+            nc.sync.dma_start(tile[:].bitcast(I32), words.rearrange("p t i -> p (t i)").bitcast(I32))
+            return tile
+
+        def zeroed_plane(width, name, engine):
+            tile = keep.tile([P, width], U8, name=name, align_bytes=64)
+            engine.memset(tile[:].bitcast(I32), 0)
+            return tile
+
+        def load_scale_rows(plane, first_row, scales):
+            passes = scales.shape[0]
+            for q in range(4):
+                rows = slice(32 * q + first_row, 32 * q + first_row + 4 * passes)
+                nc.sync.dma_start(plane[rows, :].bitcast(I32), scales[:, 4 * q : 4 * q + 4, :].bitcast(I32))
+
+        def load_rows(src, name, slot):
+            tile = loads.tile([P, PACK, src.shape[1]], F32, name=name, tag=slot, align_bytes=64)
+            nc.sync.dma_start(tile[:], src.rearrange("(p i) c -> p i c", i=PACK))
+            return tile
+
+        def gather(window, offsets, dtype, name):
+            tile = keep.tile([P, S], dtype, name=name, align_bytes=64)
+            nc.vector.tensor_copy(tile[:], window[:].indirect(offsets[:]))
+            return tile
+
+        tab2_plane = zeroed_plane(T, "tab2_plane", nc.vector)
+        w23_plane = zeroed_plane(H, "w23_plane", nc.vector)
+        tab3_plane = zeroed_plane(T, "tab3_plane", nc.vector)
+        tab_plane = zeroed_plane(T, "tab_plane", nc.vector)
+        w5_plane = zeroed_plane(2 * N, "w5_plane", nc.vector)
+        offs2_sb = load_list(offs2, "offs2_sb")
+        w2_raw = loads.tile([P, 2 * H], U8, tag="A", align_bytes=64)
+        nc.sync.dma_start(w2_raw[:].bitcast(I32), w2_words[0].bitcast(I32))
+        tab2_sb = load_table_words(tab2_words[0], "tab2_sb", "B")
+        w1_raw = {}
+        w1_raw[0, 0] = load_rows(w1[0:PASS, 0:PASS], "w1_raw00", "C")
+        load_scale_rows(tab2_plane, 0, tab2_scales)
+        load_scale_rows(w23_plane, 0, w2_scales)
+        load_scale_rows(w23_plane, 4, w3_scales)
+        b0_sb = keep.tile([P, 2, PACK], F32)
+        nc.gpsimd.dma_start(b0_sb[:], b0.rearrange("(b p t) -> p b t", b=2, t=PACK))
+
+        w2_sb = keep.tile([P, 2 * H], U8, align_bytes=64)
+        nc.vector.tensor_copy(
+            w2_sb[:].rearrange("p (b t m e) -> p b m t e", b=2, t=PACK, e=2),
+            w2_raw[:].rearrange("p (b m t e) -> p b m t e", b=2, t=PACK, e=2),
+        )
+        tab3_sb = load_table_words(tab3_words[0], "tab3_sb", "A")
+        offs3_sb = load_list(offs3, "offs3_sb")
+        offs_sb = load_list(offs, "offs_sb")
+        load_scale_rows(tab3_plane, 0, tab3_scales)
+        w3_raw = keep.tile([P, H], I32, align_bytes=64)
+        nc.sync.dma_start(w3_raw[:], w3_words[0].rearrange("p c i -> p (c i)").bitcast(I32))
+        tab_sb = [load_table_words(tab_words[a], f"tab_sb{a}", "EF"[a]) for a in range(2)]
+        load_scale_rows(tab_plane, 0, tab_scales)
+        w1_raw[1, 0] = load_rows(w1[PASS : 2 * PASS, 0:PASS], "w1_raw10", "D")
+        pos2_sb = load_list(pos2, "pos2_sb")
+        pos1_sb = load_list(pos1, "pos1_sb")
+        pos3_sb = load_list(pos3, "pos3_sb")
+        v2_words = gather(tab2_sb, offs2_sb, U32, "v2_words")
+        w1_raw[0, 1] = load_rows(w1[0:PASS, PASS : 2 * PASS], "w1_raw01", "B")
+        v2_scales = gather(tab2_plane, offs2_sb, U8, "v2_scales")
+        w23_scales = keep.tile([P, H], U8, align_bytes=64)
+        nc.vector.tensor_copy(
+            w23_scales[:].rearrange("p (b t m) -> p b t m", b=2, t=PACK),
+            w23_plane[:].rearrange("p (b m t) -> p b t m", b=2, t=PACK),
+        )
+
+        w1_codes, w1_scales, w1_bf = {}, {}, {}
+
+        def round_w1(a, b):
+            w1_bf[a, b] = rounded.tile([P, PASS * PACK], BF16, name=f"w1_bf{a}{b}", tag="bf", align_bytes=64)
+            nc.scalar.copy(
+                w1_bf[a, b][:].rearrange("p (t m i) -> p m i t", t=PACK, i=PACK),
+                w1_raw[a, b][:].rearrange("p i (m t) -> p m i t", t=PACK),
+            )
+
+        def quantize_w1(a, b):
+            w1_codes[a, b] = keep.tile([P, PASS], U32, name=f"w1_codes{a}{b}", align_bytes=64)
+            w1_scales[a, b] = keep.tile([P, PASS], U8, name=f"w1_scales{a}{b}", align_bytes=64)
+            nc.vector.quantize_mx(out=w1_codes[a, b][:].bitcast(FP8X4), scales=w1_scales[a, b][:], in_=w1_bf[a, b][:])
+
+        def first_stage(passes, name):
+            window = windows.tile([P, S], F32, name=name, tag="window")
+            for h in range(S // BANK):
+                cols = slice(h * BANK, (h + 1) * BANK)
+                acc = psum.tile([P, BANK], F32, name="acc", tag="bank")
+                for n, (lhsT, lhsT_scale, words, scales) in enumerate(passes):
+                    nc.tensor.matmul_mx(
+                        out=acc[:], lhsT=lhsT, lhsT_scale=lhsT_scale,
+                        rhs=words[:, cols].bitcast(FP8X4), rhs_scale=scales[:, cols],
+                        start=(n == 0), stop=(n == len(passes) - 1),
+                    )
+                nc.scalar.copy(window[:, cols], acc[:])
+            return window
+
+        round_w1(0, 0)
+        w1_raw[1, 1] = load_rows(w1[PASS : 2 * PASS, PASS : 2 * PASS], "w1_raw11", "C")
+        b_win = []
+        for s in range(8):
+            cols = slice(s * P, (s + 1) * P)
+            lhsT = w2_sb[:, 2 * s * P : 2 * (s + 1) * P].bitcast(FP4X4)
+            b_win.append(first_stage([(lhsT, w23_scales[:, cols], v2_words, v2_scales)], f"b{s}"))
+        round_w1(1, 0)
+
+        v3_words = gather(tab3_sb, offs3_sb, U32, "v3_words")
+        quantize_w1(0, 0)
+        v3_scales = gather(tab3_plane, offs3_sb, U8, "v3_scales")
+        w3_sb = keep.tile([P, H], I32, align_bytes=64)
+        nc.vector.tensor_copy(
+            w3_sb[:].rearrange("p (b t m) -> p b m t", b=2, t=PACK),
+            w3_raw[:].rearrange("p (b m t) -> p b m t", b=2, t=PACK),
+        )
+        v_words = [gather(tab_sb[a], offs_sb, U32, f"v_words{a}") for a in range(2)]
+        v_scales = gather(tab_plane, offs_sb, U8, "v_scales")
+        quantize_w1(1, 0)
+        w4_raw = [load_rows(w4[a * PASS : (a + 1) * PASS, :], f"w4_raw{a}", "AD"[a]) for a in range(2)]
+        w5_sb = keep.tile([P, 2, 2 * N], U8, align_bytes=64)
+        nc.sync.dma_start(w5_sb[:].bitcast(I32), w5_words.rearrange("a p c -> p a c").bitcast(I32))
+        for q in range(4):
+            nc.sync.dma_start(
+                w5_plane[32 * q : 32 * q + 4, :].bitcast(I32).rearrange("r (a n) -> r a n", a=2),
+                w5_scales[:, 4 * q : 4 * q + 4, :].bitcast(I32).rearrange("a r n -> r a n"),
+            )
+
+        w4_codes = keep.tile([P, 2 * N], U32, align_bytes=64)
+        w4_scales = keep.tile([P, 2 * N], U8, align_bytes=64)
+        w4_bf = keep.tile([P, 2 * N * PACK], BF16, align_bytes=64)
+        z_codes, z_scales = [], []
+
+        def gain_of(s):
+            b_pick = picks.tile([P, PICKS], F32, name="b_pick")
+            nc.vector.tensor_copy(b_pick[:], b_win[s][:].indirect(pos2_sb[:]))
+            gain = gains.tile([P, PICKS], F32, name="gain")
+            nc.scalar.activation(gain[:], b_pick[:], ACT.Tanh, bias=b0_sb[:, s // PACK, s % PACK : s % PACK + 1])
+            nc.scalar.activation(gain[:], gain[:], ACT.Exp)
+            return gain
+
+        def d_of(s):
+            cols = slice(s * P, (s + 1) * P)
+            return first_stage([(w3_sb[:, cols].bitcast(FP8X4), w23_scales[4:P, cols], v3_words, v3_scales)], f"d{s}")
+
+        def a_of(s):
+            b, cols = s // PACK, slice(s % PACK * P, (s % PACK + 1) * P)
+            return first_stage(
+                [(w1_codes[a, b][:, cols].bitcast(FP8X4), w1_scales[a, b][:, cols], v_words[a], v_scales[4 * a : P, :])
+                 for a in range(2)], f"a{s}")
+
+        def round_w4(a, copy):
+            copy(
+                w4_bf[:, a * N * PACK : (a + 1) * N * PACK].rearrange("p (c e i) -> p c i e", e=4, i=PACK),
+                w4_raw[a][:].rearrange("p i (c e) -> p c i e", e=4),
+            )
+
+        z_f32 = []
+
+        def quantize_z(b, copy):
+            z_bf = rounded.tile([P, PICKS * PACK], BF16, name="z_bf", tag="bf", align_bytes=64)
+            copy(
+                z_bf[:].rearrange("p (c e t) -> p c t e", e=4, t=PACK),
+                z_f32[b][:].rearrange("p t (c e) -> p c t e", e=4),
+            )
+            z_codes.append(keep.tile([P, PICKS], U32, name=f"z_codes{b}", align_bytes=64))
+            z_scales.append(keep.tile([P, PICKS], U8, name=f"z_scales{b}", align_bytes=64))
+            nc.vector.quantize_mx(out=z_codes[b][:].bitcast(FP8X4), scales=z_scales[b][:], in_=z_bf[:])
+
+        GAIN_AHEAD, D_AHEAD = 2, 2
+        d_win = {s: d_of(s) for s in range(D_AHEAD)}
+        round_w1(0, 1)
+        quantize_w1(0, 1)
+        gain = {s: gain_of(s) for s in range(GAIN_AHEAD)}
+        for s in range(8):
+            b, t = divmod(s, PACK)
+            a_win = a_of(s)
+            if s + GAIN_AHEAD < 8:
+                gain[s + GAIN_AHEAD] = gain_of(s + GAIN_AHEAD)
+            if s + D_AHEAD < 8:
+                d_win[s + D_AHEAD] = d_of(s + D_AHEAD)
+            if s == -1:
+                round_w1(0, 1)
+                quantize_w1(0, 1)
+            if s == 1:
+                round_w1(1, 1)
+                quantize_w1(1, 1)
+            if t == 0:
+                z_f32.append(joined.tile([P, PACK, PICKS], F32, name="z_f32"))
+            scaled = picks.tile([P, PICKS], F32, name="scaled")
+            nc.vector.tensor_tensor(scaled[:], a_win[:].indirect(pos1_sb[:]), gain[s][:], ALU.mult)
+            nc.vector.tensor_tensor(z_f32[b][:, t, :], d_win[s][:].indirect(pos3_sb[:]), scaled[:], ALU.add)
+            if s == 4:
+                round_w4(0, nc.vector.tensor_copy)
+            if s == 5:
+                round_w4(1, nc.vector.tensor_copy)
+            if s == 6:
+                for lo, hi in ((0, 512), (512, 768)):
+                    nc.vector.quantize_mx(
+                        out=w4_codes[:, lo:hi].bitcast(FP8X4), scales=w4_scales[:, lo:hi],
+                        in_=w4_bf[:, PACK * lo : PACK * hi])
+            if s == 5:
+                quantize_z(0, nc.scalar.copy)
+        quantize_z(1, nc.vector.tensor_copy)
+
+        y1 = [psum.tile([P, PICKS], F32, name=f"y1_{n}", tag="bank") for n in range(N // P)]
+        y2 = [psum.tile([P, PICKS], F32, name=f"y2_{n}", tag="bank") for n in range(N // P)]
+        for a in range(2):
+            for n in range(N // P):
+                cols = slice(a * N + n * P, a * N + (n + 1) * P)
+                nc.tensor.matmul_mx(
+                    out=y2[n][:], lhsT=w5_sb[:, a, 2 * n * P : 2 * (n + 1) * P].bitcast(FP4X4),
+                    lhsT_scale=w5_plane[:, cols], rhs=z_codes[a][:].bitcast(FP8X4), rhs_scale=z_scales[a][:],
+                    start=(a == 0), stop=(a == 1))
+                nc.tensor.matmul_mx(
+                    out=y1[n][:], lhsT=w4_codes[:, cols].bitcast(FP8X4), lhsT_scale=w4_scales[:, cols],
+                    rhs=z_codes[a][:].bitcast(FP8X4), rhs_scale=z_scales[a][:],
+                    start=(a == 0), stop=(a == 1))
+        for n in range(N // P):
+            squared = picks.tile([P, PICKS], F32, name="b_pick")
+            nc.scalar.activation(squared[:], y2[n][:], ACT.Square)
+            result = picks.tile([P, PICKS], F32, name="scaled")
+            nc.vector.tensor_tensor(result[:], y1[n][:], squared[:], ALU.subtract)
+            nc.sync.dma_start(out[n * P : (n + 1) * P, :], result[:])

@@ -20,6 +20,9 @@ P = 128
 PACK = 4
 PASS = P * PACK
 BANK = 512
+RING = 3
+PIECE = 256
+HF = 0
 
 
 def tile_list_roast_profile_join_kernel(
@@ -49,7 +52,7 @@ def tile_list_roast_profile_join_kernel(
             return tile
 
         def zeroed_plane(width, name, engine):
-            tile = keep.tile([P, width], U8, name=name, align_bytes=64)
+            tile = keep.tile([P, width], U8, name=name, tag=name, align_bytes=64)
             engine.memset(tile[:].bitcast(I32), 0)
             return tile
 
@@ -69,66 +72,75 @@ def tile_list_roast_profile_join_kernel(
             nc.vector.tensor_copy(tile[:], window[:].indirect(offsets[:]))
             return tile
 
+        def deal_scales(plane, name):
+            tile = keep.tile([P, H], U8, name=name, align_bytes=64)
+            nc.vector.tensor_copy(
+                tile[:].rearrange("p (b t m) -> p b t m", b=2, t=PACK),
+                plane[:].rearrange("p (b m t) -> p b t m", b=2, t=PACK),
+            )
+            return tile
+
         tab2_plane = zeroed_plane(T, "tab2_plane", nc.vector)
-        w23_plane = zeroed_plane(H, "w23_plane", nc.vector)
+        w2_plane = zeroed_plane(H, "w2_plane", nc.vector)
         tab3_plane = zeroed_plane(T, "tab3_plane", nc.vector)
+        w3_plane = zeroed_plane(H, "w3_plane", nc.vector)
         tab_plane = zeroed_plane(T, "tab_plane", nc.vector)
         w5_plane = zeroed_plane(2 * N, "w5_plane", nc.vector)
         offs2_sb = load_list(offs2, "offs2_sb")
-        w2_raw = loads.tile([P, 2 * H], U8, tag="A", align_bytes=64)
+        w2_raw = keep.tile([P, 2 * H], U8, align_bytes=64)
         nc.sync.dma_start(w2_raw[:].bitcast(I32), w2_words[0].bitcast(I32))
+        offs3_sb = load_list(offs3, "offs3_sb")
+        load_scale_rows(tab2_plane, 0, tab2_scales)
         tab2_sb = load_table_words(tab2_words[0], "tab2_sb", "B")
         w1_raw = {}
-        w1_raw[0, 0] = load_rows(w1[0:PASS, 0:PASS], "w1_raw00", "C")
-        load_scale_rows(tab2_plane, 0, tab2_scales)
-        load_scale_rows(w23_plane, 0, w2_scales)
-        load_scale_rows(w23_plane, 4, w3_scales)
-        b0_sb = keep.tile([P, 2, PACK], F32)
-        nc.gpsimd.dma_start(b0_sb[:], b0.rearrange("(b p t) -> p b t", b=2, t=PACK))
+        w1_raw[0, 0] = [load_rows(w1[0:PASS, 0:PASS], "w1_raw00", "C")]
+        load_scale_rows(w2_plane, 0, w2_scales)
 
         w2_sb = keep.tile([P, 2 * H], U8, align_bytes=64)
         nc.vector.tensor_copy(
-            w2_sb[:].rearrange("p (b t m e) -> p b m t e", b=2, t=PACK, e=2),
-            w2_raw[:].rearrange("p (b m t e) -> p b m t e", b=2, t=PACK, e=2),
+            w2_sb[:].bitcast(U16).rearrange("p (b t m) -> p b m t", b=2, t=PACK),
+            w2_raw[:].bitcast(U16).rearrange("p (b m t) -> p b m t", b=2, t=PACK),
         )
         tab3_sb = load_table_words(tab3_words[0], "tab3_sb", "A")
-        offs3_sb = load_list(offs3, "offs3_sb")
-        offs_sb = load_list(offs, "offs_sb")
         load_scale_rows(tab3_plane, 0, tab3_scales)
         w3_raw = keep.tile([P, H], I32, align_bytes=64)
         nc.sync.dma_start(w3_raw[:], w3_words[0].rearrange("p c i -> p (c i)").bitcast(I32))
-        tab_sb = [load_table_words(tab_words[a], f"tab_sb{a}", "EF"[a]) for a in range(2)]
+        tab_sb = [load_table_words(tab_words[0], "tab_sb0", "E")]
+        load_scale_rows(w3_plane, 0, w3_scales)
+        offs_sb = load_list(offs, "offs_sb")
+        w1_raw[1, 0] = [load_rows(w1[PASS : 2 * PASS, 0:PASS], "w1_raw10", "D")]
+        tab_sb.append(load_table_words(tab_words[1], "tab_sb1", "F"))
         load_scale_rows(tab_plane, 0, tab_scales)
-        w1_raw[1, 0] = load_rows(w1[PASS : 2 * PASS, 0:PASS], "w1_raw10", "D")
+        v2_scales = gather(tab2_plane, offs2_sb, U8, "v2_scales")
+        v2_words = gather(tab2_sb, offs2_sb, U32, "v2_words")
+        w2_dealt = deal_scales(w2_plane, "w2_dealt")
+
+        w1_raw[0, 1] = [load_rows(w1[0:PASS, PASS : 2 * PASS], "w1_raw01", "B")]
         pos2_sb = load_list(pos2, "pos2_sb")
+        b0_sb = keep.tile([P, 2, PACK], F32)
+        nc.sync.dma_start(b0_sb[:], b0.rearrange("(b p t) -> p b t", b=2, t=PACK))
         pos1_sb = load_list(pos1, "pos1_sb")
         pos3_sb = load_list(pos3, "pos3_sb")
-        v2_words = gather(tab2_sb, offs2_sb, U32, "v2_words")
-        w1_raw[0, 1] = load_rows(w1[0:PASS, PASS : 2 * PASS], "w1_raw01", "B")
-        v2_scales = gather(tab2_plane, offs2_sb, U8, "v2_scales")
-        w23_scales = keep.tile([P, H], U8, align_bytes=64)
-        nc.vector.tensor_copy(
-            w23_scales[:].rearrange("p (b t m) -> p b t m", b=2, t=PACK),
-            w23_plane[:].rearrange("p (b m t) -> p b t m", b=2, t=PACK),
-        )
-
         w1_codes, w1_scales, w1_bf = {}, {}, {}
 
         def round_w1(a, b):
-            w1_bf[a, b] = rounded.tile([P, PASS * PACK], BF16, name=f"w1_bf{a}{b}", tag="bf", align_bytes=64)
-            nc.scalar.copy(
-                w1_bf[a, b][:].rearrange("p (t m i) -> p m i t", t=PACK, i=PACK),
-                w1_raw[a, b][:].rearrange("p i (m t) -> p m i t", t=PACK),
-            )
+            pool, slot = (keep, "w1_bf10") if (a, b) == (1, 0) else (rounded, "bf")
+            w1_bf[a, b] = pool.tile([P, PASS * PACK], BF16, name=f"w1_bf{a}{b}", tag=slot, align_bytes=64)
+            dealt = w1_bf[a, b][:].rearrange("p (t m i) -> p m i t", t=PACK, i=PACK)
+            width = P // len(w1_raw[a, b])
+            for n, raw in enumerate(w1_raw[a, b]):
+                nc.scalar.copy(dealt[:, n * width : (n + 1) * width], raw[:].rearrange("p i (m t) -> p m i t", t=PACK))
 
         def quantize_w1(a, b):
-            w1_codes[a, b] = keep.tile([P, PASS], U32, name=f"w1_codes{a}{b}", align_bytes=64)
+            slot = "tab_plane" if (a, b) == (1, 0) else f"w1_codes{a}{b}"
+            w1_codes[a, b] = keep.tile([P, PASS], U32, name=f"w1_codes{a}{b}", tag=slot, align_bytes=64)
             w1_scales[a, b] = keep.tile([P, PASS], U8, name=f"w1_scales{a}{b}", align_bytes=64)
             nc.vector.quantize_mx(out=w1_codes[a, b][:].bitcast(FP8X4), scales=w1_scales[a, b][:], in_=w1_bf[a, b][:])
 
-        def first_stage(passes, name):
-            window = windows.tile([P, S], F32, name=name, tag="window")
-            for h in range(S // BANK):
+        def first_stage(passes, name, halves=(0, 1), window=None):
+            if window is None:
+                window = windows.tile([P, S], F32, name=name, tag="window")
+            for h in halves:
                 cols = slice(h * BANK, (h + 1) * BANK)
                 acc = psum.tile([P, BANK], F32, name="acc", tag="bank")
                 for n, (lhsT, lhsT_scale, words, scales) in enumerate(passes):
@@ -141,13 +153,14 @@ def tile_list_roast_profile_join_kernel(
             return window
 
         round_w1(0, 0)
-        w1_raw[1, 1] = load_rows(w1[PASS : 2 * PASS, PASS : 2 * PASS], "w1_raw11", "C")
-        b_win = []
-        for s in range(8):
+        w1_raw[1, 1] = [load_rows(w1[PASS : 2 * PASS, PASS : 2 * PASS], "w1_raw11", "C")]
+        b_win = {}
+        for h, s in [(0, s) for s in range(HF)] + [(1, s) for s in range(HF)] + [(h, s) for s in range(HF, 8) for h in range(2)]:
             cols = slice(s * P, (s + 1) * P)
             lhsT = w2_sb[:, 2 * s * P : 2 * (s + 1) * P].bitcast(FP4X4)
-            b_win.append(first_stage([(lhsT, w23_scales[:, cols], v2_words, v2_scales)], f"b{s}"))
-        round_w1(1, 0)
+            b_win[s] = first_stage([(lhsT, w2_dealt[:, cols], v2_words, v2_scales)], f"b{s}", (h,), b_win.get(s))
+            if (s, h) == (4, 1):
+                round_w1(1, 0)
 
         v3_words = gather(tab3_sb, offs3_sb, U32, "v3_words")
         quantize_w1(0, 0)
@@ -157,9 +170,11 @@ def tile_list_roast_profile_join_kernel(
             w3_sb[:].rearrange("p (b t m) -> p b m t", b=2, t=PACK),
             w3_raw[:].rearrange("p (b m t) -> p b m t", b=2, t=PACK),
         )
+        w3_dealt = deal_scales(w3_plane, "w3_dealt")
         v_words = [gather(tab_sb[a], offs_sb, U32, f"v_words{a}") for a in range(2)]
         v_scales = gather(tab_plane, offs_sb, U8, "v_scales")
         quantize_w1(1, 0)
+        b_picks = keep.tile([P, RING, PICKS], F32, tag="w1_bf10", align_bytes=64)
         w4_raw = [load_rows(w4[a * PASS : (a + 1) * PASS, :], f"w4_raw{a}", "AD"[a]) for a in range(2)]
         w5_sb = keep.tile([P, 2, 2 * N], U8, align_bytes=64)
         nc.sync.dma_start(w5_sb[:].bitcast(I32), w5_words.rearrange("a p c -> p a c").bitcast(I32))
@@ -175,16 +190,16 @@ def tile_list_roast_profile_join_kernel(
         z_codes, z_scales = [], []
 
         def gain_of(s):
-            b_pick = picks.tile([P, PICKS], F32, name="b_pick")
-            nc.vector.tensor_copy(b_pick[:], b_win[s][:].indirect(pos2_sb[:]))
+            b_pick = b_picks[:, s % RING, :]
+            nc.vector.tensor_copy(b_pick, b_win[s][:].indirect(pos2_sb[:]))
             gain = gains.tile([P, PICKS], F32, name="gain")
-            nc.scalar.activation(gain[:], b_pick[:], ACT.Tanh, bias=b0_sb[:, s // PACK, s % PACK : s % PACK + 1])
+            nc.scalar.activation(gain[:], b_pick, ACT.Tanh, bias=b0_sb[:, s // PACK, s % PACK : s % PACK + 1])
             nc.scalar.activation(gain[:], gain[:], ACT.Exp)
             return gain
 
         def d_of(s):
             cols = slice(s * P, (s + 1) * P)
-            return first_stage([(w3_sb[:, cols].bitcast(FP8X4), w23_scales[4:P, cols], v3_words, v3_scales)], f"d{s}")
+            return first_stage([(w3_sb[:, cols].bitcast(FP8X4), w3_dealt[:, cols], v3_words, v3_scales)], f"d{s}")
 
         def a_of(s):
             b, cols = s // PACK, slice(s % PACK * P, (s % PACK + 1) * P)
@@ -200,51 +215,58 @@ def tile_list_roast_profile_join_kernel(
 
         z_f32 = []
 
-        def quantize_z(b, copy):
-            z_bf = rounded.tile([P, PICKS * PACK], BF16, name="z_bf", tag="bf", align_bytes=64)
+        z_bf = []
+
+        def round_z(b, lo, hi, copy):
+            if lo == 0:
+                z_bf.append(rounded.tile([P, PICKS * PACK], BF16, name="z_bf", tag="bf", align_bytes=64))
             copy(
-                z_bf[:].rearrange("p (c e t) -> p c t e", e=4, t=PACK),
-                z_f32[b][:].rearrange("p t (c e) -> p c t e", e=4),
+                z_bf[b][:, PACK * lo : PACK * hi].rearrange("p (c e t) -> p c t e", e=4, t=PACK),
+                z_f32[b][:, :, lo:hi].rearrange("p t (c e) -> p c t e", e=4),
             )
+
+        def quantize_z(b):
             z_codes.append(keep.tile([P, PICKS], U32, name=f"z_codes{b}", align_bytes=64))
             z_scales.append(keep.tile([P, PICKS], U8, name=f"z_scales{b}", align_bytes=64))
-            nc.vector.quantize_mx(out=z_codes[b][:].bitcast(FP8X4), scales=z_scales[b][:], in_=z_bf[:])
+            nc.vector.quantize_mx(out=z_codes[b][:].bitcast(FP8X4), scales=z_scales[b][:], in_=z_bf[b][:])
 
-        GAIN_AHEAD, D_AHEAD = 2, 2
-        d_win = {s: d_of(s) for s in range(D_AHEAD)}
-        round_w1(0, 1)
-        quantize_w1(0, 1)
-        gain = {s: gain_of(s) for s in range(GAIN_AHEAD)}
-        for s in range(8):
-            b, t = divmod(s, PACK)
-            a_win = a_of(s)
-            if s + GAIN_AHEAD < 8:
-                gain[s + GAIN_AHEAD] = gain_of(s + GAIN_AHEAD)
-            if s + D_AHEAD < 8:
-                d_win[s + D_AHEAD] = d_of(s + D_AHEAD)
-            if s == -1:
-                round_w1(0, 1)
-                quantize_w1(0, 1)
-            if s == 1:
-                round_w1(1, 1)
-                quantize_w1(1, 1)
-            if t == 0:
-                z_f32.append(joined.tile([P, PACK, PICKS], F32, name="z_f32"))
+        def scale_a(s, a_win, gain):
             scaled = picks.tile([P, PICKS], F32, name="scaled")
-            nc.vector.tensor_tensor(scaled[:], a_win[:].indirect(pos1_sb[:]), gain[s][:], ALU.mult)
-            nc.vector.tensor_tensor(z_f32[b][:, t, :], d_win[s][:].indirect(pos3_sb[:]), scaled[:], ALU.add)
+            nc.vector.tensor_tensor(scaled[:], a_win[:].indirect(pos1_sb[:]), gain[:], ALU.mult)
+            return scaled
+
+        def shift_by_d(s, d_win, scaled, lo, hi):
+            b, t = divmod(s, PACK)
+            if t == 0 and lo == 0:
+                z_f32.append(joined.tile([P, PACK, PICKS], F32, name="z_f32"))
+            nc.vector.tensor_tensor(
+                z_f32[b][:, t, lo:hi], d_win[:].indirect(pos3_sb[:, lo // 16 : hi // 16]), scaled[:, lo:hi], ALU.add)
+
+        for a in range(2):
+            round_w1(a, 1)
+            quantize_w1(a, 1)
+        round_w4(1, nc.vector.tensor_copy)
+        scaled = {}
+        for s in range(8):
+            a_win = a_of(s)
+            scaled[s] = scale_a(s, a_win, gain_of(s))
+            if s > 0:
+                shift_by_d(s - 1, d_of(s - 1), scaled[s - 1], 0, PICKS)
             if s == 4:
                 round_w4(0, nc.vector.tensor_copy)
-            if s == 5:
-                round_w4(1, nc.vector.tensor_copy)
-            if s == 6:
                 for lo, hi in ((0, 512), (512, 768)):
                     nc.vector.quantize_mx(
                         out=w4_codes[:, lo:hi].bitcast(FP8X4), scales=w4_scales[:, lo:hi],
                         in_=w4_bf[:, PACK * lo : PACK * hi])
-            if s == 5:
-                quantize_z(0, nc.scalar.copy)
-        quantize_z(1, nc.vector.tensor_copy)
+            if s == 7:
+                round_z(0, 0, PICKS, nc.scalar.copy)
+                quantize_z(0)
+        d_win = d_of(7)
+        shift_by_d(7, d_win, scaled[7], 0, PICKS // 2)
+        round_z(1, 0, PICKS // 2, nc.scalar.copy)
+        shift_by_d(7, d_win, scaled[7], PICKS // 2, PICKS)
+        round_z(1, PICKS // 2, PICKS, nc.vector.tensor_copy)
+        quantize_z(1)
 
         y1 = [psum.tile([P, PICKS], F32, name=f"y1_{n}", tag="bank") for n in range(N // P)]
         y2 = [psum.tile([P, PICKS], F32, name=f"y2_{n}", tag="bank") for n in range(N // P)]
@@ -260,8 +282,10 @@ def tile_list_roast_profile_join_kernel(
                     rhs=z_codes[a][:].bitcast(FP8X4), rhs_scale=z_scales[a][:],
                     start=(a == 0), stop=(a == 1))
         for n in range(N // P):
-            squared = picks.tile([P, PICKS], F32, name="b_pick")
-            nc.scalar.activation(squared[:], y2[n][:], ACT.Square)
+            squared = picks.tile([P, PICKS], F32, name="b_pick", bufs=3)
             result = picks.tile([P, PICKS], F32, name="scaled")
-            nc.vector.tensor_tensor(result[:], y1[n][:], squared[:], ALU.subtract)
-            nc.sync.dma_start(out[n * P : (n + 1) * P, :], result[:])
+            for lo in range(0, PICKS, PIECE):
+                cols = slice(lo, lo + PIECE)
+                nc.scalar.activation(squared[:, cols], y2[n][:, cols], ACT.Square)
+                nc.vector.tensor_tensor(result[:, cols], y1[n][:, cols], squared[:, cols], ALU.subtract)
+                nc.sync.dma_start(out[n * P : (n + 1) * P, cols], result[:, cols])

@@ -35,7 +35,7 @@ def tile_list_roast_profile_join_kernel(
         keep = ctx.enter_context(tc.tile_pool(name="keep", bufs=1))
         loads = ctx.enter_context(tc.tile_pool(name="loads", bufs=1))
         rounded = ctx.enter_context(tc.tile_pool(name="rounded", bufs=2))
-        windows = ctx.enter_context(tc.tile_pool(name="windows", bufs=14))
+        windows = ctx.enter_context(tc.tile_pool(name="windows", bufs=13))
         picks = ctx.enter_context(tc.tile_pool(name="picks", bufs=3))
         gains = ctx.enter_context(tc.tile_pool(name="gains", bufs=6))
         joined = ctx.enter_context(tc.tile_pool(name="joined", bufs=2))
@@ -102,15 +102,15 @@ def tile_list_roast_profile_join_kernel(
             w2_raw[:].bitcast(U16).rearrange("p (b m t) -> p b m t", b=2, t=PACK),
         )
         tab3_sb = load_table_words(tab3_words[0], "tab3_sb", "A")
-        load_scale_rows(tab3_plane, 0, tab3_scales)
+        load_scale_rows(tab3_plane, 4, tab3_scales)
         w3_raw = keep.tile([P, H], I32, align_bytes=64)
         nc.sync.dma_start(w3_raw[:], w3_words[0].rearrange("p c i -> p (c i)").bitcast(I32))
         tab_sb = [load_table_words(tab_words[0], "tab_sb0", "E")]
-        load_scale_rows(w3_plane, 0, w3_scales)
+        load_scale_rows(w3_plane, 8, w3_scales)
         offs_sb = load_list(offs, "offs_sb")
         w1_raw[1, 0] = [load_rows(w1[PASS : 2 * PASS, 0:PASS], "w1_raw10", "D")]
         tab_sb.append(load_table_words(tab_words[1], "tab_sb1", "F"))
-        load_scale_rows(tab_plane, 0, tab_scales)
+        load_scale_rows(tab_plane, 8, tab_scales)
         v2_scales = gather(tab2_plane, offs2_sb, U8, "v2_scales")
         v2_words = gather(tab2_sb, offs2_sb, U32, "v2_words")
         w2_dealt = deal_scales(w2_plane, "w2_dealt")
@@ -139,7 +139,8 @@ def tile_list_roast_profile_join_kernel(
 
         def first_stage(passes, name, halves=(0, 1), window=None):
             if window is None:
-                window = windows.tile([P, S], F32, name=name, tag="window")
+                pool, slot = (keep, "a7") if name == "a7" else (windows, "window")
+                window = pool.tile([P, S], F32, name=name, tag=slot, align_bytes=64)
             for h in halves:
                 cols = slice(h * BANK, (h + 1) * BANK)
                 acc = psum.tile([P, BANK], F32, name="acc", tag="bank")
@@ -199,12 +200,12 @@ def tile_list_roast_profile_join_kernel(
 
         def d_of(s):
             cols = slice(s * P, (s + 1) * P)
-            return first_stage([(w3_sb[:, cols].bitcast(FP8X4), w3_dealt[:, cols], v3_words, v3_scales)], f"d{s}")
+            return first_stage([(w3_sb[:, cols].bitcast(FP8X4), w3_dealt[8:P, cols], v3_words, v3_scales[4:P, :])], f"d{s}")
 
         def a_of(s):
             b, cols = s // PACK, slice(s % PACK * P, (s % PACK + 1) * P)
             return first_stage(
-                [(w1_codes[a, b][:, cols].bitcast(FP8X4), w1_scales[a, b][:, cols], v_words[a], v_scales[4 * a : P, :])
+                [(w1_codes[a, b][:, cols].bitcast(FP8X4), w1_scales[a, b][:, cols], v_words[a], v_scales[8 + 4 * a : P, :])
                  for a in range(2)], f"a{s}")
 
         def round_w4(a, copy):
@@ -226,7 +227,7 @@ def tile_list_roast_profile_join_kernel(
             )
 
         def quantize_z(b):
-            z_codes.append(keep.tile([P, PICKS], U32, name=f"z_codes{b}", align_bytes=64))
+            z_codes.append(keep.tile([P, PICKS], U32, name=f"z_codes{b}", tag=("a7", "z_codes1")[b], align_bytes=64))
             z_scales.append(keep.tile([P, PICKS], U8, name=f"z_scales{b}", align_bytes=64))
             nc.vector.quantize_mx(out=z_codes[b][:].bitcast(FP8X4), scales=z_scales[b][:], in_=z_bf[b][:])
 
@@ -258,8 +259,9 @@ def tile_list_roast_profile_join_kernel(
                     nc.vector.quantize_mx(
                         out=w4_codes[:, lo:hi].bitcast(FP8X4), scales=w4_scales[:, lo:hi],
                         in_=w4_bf[:, PACK * lo : PACK * hi])
+            if s == 5:
+                round_z(0, 0, PICKS, nc.vector.tensor_copy)
             if s == 7:
-                round_z(0, 0, PICKS, nc.scalar.copy)
                 quantize_z(0)
         d_win = d_of(7)
         shift_by_d(7, d_win, scaled[7], 0, PICKS // 2)

@@ -34,7 +34,7 @@ def tile_list_roast_profile_join_kernel(
         lists = ctx.enter_context(tc.tile_pool(name="lists", bufs=1))
         keep = ctx.enter_context(tc.tile_pool(name="keep", bufs=1))
         loads = ctx.enter_context(tc.tile_pool(name="loads", bufs=1))
-        rounded = ctx.enter_context(tc.tile_pool(name="rounded", bufs=2))
+        rounded = ctx.enter_context(tc.tile_pool(name="rounded", bufs=3))
         windows = ctx.enter_context(tc.tile_pool(name="windows", bufs=13))
         picks = ctx.enter_context(tc.tile_pool(name="picks", bufs=3))
         gains = ctx.enter_context(tc.tile_pool(name="gains", bufs=6))
@@ -126,14 +126,20 @@ def tile_list_roast_profile_join_kernel(
         def round_w1(a, b):
             pool, slot = (keep, "w1_bf10") if (a, b) == (1, 0) else (rounded, "bf")
             w1_bf[a, b] = pool.tile([P, PASS * PACK], BF16, name=f"w1_bf{a}{b}", tag=slot, align_bytes=64)
-            dealt = w1_bf[a, b][:].rearrange("p (t m i) -> p m i t", t=PACK, i=PACK)
-            width = P // len(w1_raw[a, b])
-            for n, raw in enumerate(w1_raw[a, b]):
-                nc.scalar.copy(dealt[:, n * width : (n + 1) * width], raw[:].rearrange("p i (m t) -> p m i t", t=PACK))
+            if (a, b) in ((1, 0), (0, 1)):
+                dealt = w1_bf[a, b][:].rearrange("p (t m i) -> p t m i", t=PACK, i=PACK)
+                raw = w1_raw[a, b][0][:].rearrange("p i (m t) -> p t m i", t=PACK)
+                for t in range(PACK):
+                    nc.gpsimd.tensor_scalar(dealt[:, t], raw[:, t], 1.0, 0.0, ALU.mult, ALU.add)
+            else:
+                nc.scalar.copy(
+                    w1_bf[a, b][:].rearrange("p (t m i) -> p m i t", t=PACK, i=PACK),
+                    w1_raw[a, b][0][:].rearrange("p i (m t) -> p m i t", t=PACK),
+                )
 
         def quantize_w1(a, b):
-            slot = "tab_plane" if (a, b) == (1, 0) else f"w1_codes{a}{b}"
-            w1_codes[a, b] = keep.tile([P, PASS], U32, name=f"w1_codes{a}{b}", tag=slot, align_bytes=64)
+            pool, slot = {(1, 0): (keep, "tab_plane"), (0, 1): (loads, "A")}.get((a, b), (keep, f"w1_codes{a}{b}"))
+            w1_codes[a, b] = pool.tile([P, PASS], U32, name=f"w1_codes{a}{b}", tag=slot, align_bytes=64)
             w1_scales[a, b] = keep.tile([P, PASS], U8, name=f"w1_scales{a}{b}", align_bytes=64)
             nc.vector.quantize_mx(out=w1_codes[a, b][:].bitcast(FP8X4), scales=w1_scales[a, b][:], in_=w1_bf[a, b][:])
 
@@ -243,18 +249,24 @@ def tile_list_roast_profile_join_kernel(
             nc.vector.tensor_tensor(
                 z_f32[b][:, t, lo:hi], d_win[:].indirect(pos3_sb[:, lo // 16 : hi // 16]), scaled[:, lo:hi], ALU.add)
 
-        for a in range(2):
-            round_w1(a, 1)
-            quantize_w1(a, 1)
-        round_w4(1, nc.vector.tensor_copy)
+        round_w1(0, 1)
+        d_win = {s: d_of(s) for s in range(3)}
+        round_w1(1, 1)
+        quantize_w1(1, 1)
         scaled = {}
         for s in range(8):
             a_win = a_of(s)
             scaled[s] = scale_a(s, a_win, gain_of(s))
             if s > 0:
-                shift_by_d(s - 1, d_of(s - 1), scaled[s - 1], 0, PICKS)
+                if s - 1 not in d_win:
+                    d_win[s - 1] = d_of(s - 1)
+                shift_by_d(s - 1, d_win[s - 1], scaled[s - 1], 0, PICKS)
+            if s == 0:
+                round_w4(0, nc.scalar.copy)
+                quantize_w1(0, 1)
+            if s == 2:
+                round_w4(1, nc.scalar.copy)
             if s == 4:
-                round_w4(0, nc.vector.tensor_copy)
                 for lo, hi in ((0, 512), (512, 768)):
                     nc.vector.quantize_mx(
                         out=w4_codes[:, lo:hi].bitcast(FP8X4), scales=w4_scales[:, lo:hi],
@@ -263,10 +275,10 @@ def tile_list_roast_profile_join_kernel(
                 round_z(0, 0, PICKS, nc.vector.tensor_copy)
             if s == 7:
                 quantize_z(0)
-        d_win = d_of(7)
-        shift_by_d(7, d_win, scaled[7], 0, PICKS // 2)
+        last = d_of(7)
+        shift_by_d(7, last, scaled[7], 0, PICKS // 2)
         round_z(1, 0, PICKS // 2, nc.scalar.copy)
-        shift_by_d(7, d_win, scaled[7], PICKS // 2, PICKS)
+        shift_by_d(7, last, scaled[7], PICKS // 2, PICKS)
         round_z(1, PICKS // 2, PICKS, nc.vector.tensor_copy)
         quantize_z(1)
 

from contextlib import ExitStack

import concourse.mybir as mybir

K, K2, H, N, T, S, PICKS = 1024, 512, 1024, 384, 2048, 1024, 512
FLOPS = 2 * S * H * (K + 2 * K2) + 2 * 2 * H * N * PICKS

F32 = mybir.dt.float32
BF16 = mybir.dt.bfloat16
I32 = mybir.dt.int32
U32 = mybir.dt.uint32
U16 = mybir.dt.uint16
U8 = mybir.dt.uint8
FP8X4 = mybir.dt.float8_e4m3fn_x4
FP4X4 = mybir.dt.float4_e2m1fn_x4
ACT = mybir.ActivationFunctionType
ALU = mybir.AluOpType

P = 128
PACK = 4
PASS = P * PACK
BANK = 512
RING = 3
PIECE = 256
HF = 0


def tile_list_roast_profile_join_kernel(
    tc, tab_words, tab_scales, tab2_words, tab2_scales, tab3_words, tab3_scales, offs, offs2, offs3,
    pos1, pos2, pos3, w1, w2_words, w2_scales, b0, w3_words, w3_scales, w4, w5_words, w5_scales, out,
):
    nc = tc.nc
    with ExitStack() as ctx:
        lists = ctx.enter_context(tc.tile_pool(name="lists", bufs=1))
        keep = ctx.enter_context(tc.tile_pool(name="keep", bufs=1))
        loads = ctx.enter_context(tc.tile_pool(name="loads", bufs=1))
        rounded = ctx.enter_context(tc.tile_pool(name="rounded", bufs=3))
        windows = ctx.enter_context(tc.tile_pool(name="windows", bufs=13))
        picks = ctx.enter_context(tc.tile_pool(name="picks", bufs=3))
        gains = ctx.enter_context(tc.tile_pool(name="gains", bufs=6))
        joined = ctx.enter_context(tc.tile_pool(name="joined", bufs=2))
        psum = ctx.enter_context(tc.psum_pool(name="psum", bufs=8))

        def load_list(src, name):
            tile = lists.tile(list(src.shape), U16, name=name)
            nc.sync.dma_start(tile[:], src)
            return tile

        def load_table_words(words, name, slot):
            tile = loads.tile([P, T], U32, name=name, tag=slot, align_bytes=64)
            nc.sync.dma_start(tile[:].bitcast(I32), words.rearrange("p t i -> p (t i)").bitcast(I32))
            return tile

        def zeroed_plane(width, name, engine):
            tile = keep.tile([P, width], U8, name=name, tag=name, align_bytes=64)
            engine.memset(tile[:].bitcast(I32), 0)
            return tile

        def load_scale_rows(plane, first_row, scales):
            passes = scales.shape[0]
            for q in range(4):
                rows = slice(32 * q + first_row, 32 * q + first_row + 4 * passes)
                nc.sync.dma_start(plane[rows, :].bitcast(I32), scales[:, 4 * q : 4 * q + 4, :].bitcast(I32))

        def load_rows(src, name, slot):
            tile = loads.tile([P, PACK, src.shape[1]], F32, name=name, tag=slot, align_bytes=64)
            nc.sync.dma_start(tile[:], src.rearrange("(p i) c -> p i c", i=PACK))
            return tile

        def gather(window, offsets, dtype, name):
            tile = keep.tile([P, S], dtype, name=name, align_bytes=64)
            nc.vector.tensor_copy(tile[:], window[:].indirect(offsets[:]))
            return tile

        def deal_scales(plane, name):
            tile = keep.tile([P, H], U8, name=name, align_bytes=64)
            nc.vector.tensor_copy(
                tile[:].rearrange("p (b t m) -> p b t m", b=2, t=PACK),
                plane[:].rearrange("p (b m t) -> p b t m", b=2, t=PACK),
            )
            return tile

        tab2_plane = zeroed_plane(T, "tab2_plane", nc.vector)
        w2_plane = zeroed_plane(H, "w2_plane", nc.vector)
        tab3_plane = zeroed_plane(T, "tab3_plane", nc.vector)
        w3_plane = zeroed_plane(H, "w3_plane", nc.vector)
        tab_plane = zeroed_plane(T, "tab_plane", nc.vector)
        w5_plane = zeroed_plane(2 * N, "w5_plane", nc.vector)
        offs2_sb = load_list(offs2, "offs2_sb")
        w2_raw = keep.tile([P, 2 * H], U8, align_bytes=64)
        nc.sync.dma_start(w2_raw[:].bitcast(I32), w2_words[0].bitcast(I32))
        offs3_sb = load_list(offs3, "offs3_sb")
        load_scale_rows(tab2_plane, 0, tab2_scales)
        tab2_sb = load_table_words(tab2_words[0], "tab2_sb", "B")
        w1_raw = {}
        w1_raw[0, 0] = [load_rows(w1[0:PASS, 0:PASS], "w1_raw00", "C")]
        load_scale_rows(w2_plane, 0, w2_scales)

        w2_sb = keep.tile([P, 2 * H], U8, align_bytes=64)
        nc.vector.tensor_copy(
            w2_sb[:].bitcast(U16).rearrange("p (b t m) -> p b m t", b=2, t=PACK),
            w2_raw[:].bitcast(U16).rearrange("p (b m t) -> p b m t", b=2, t=PACK),
        )
        tab3_sb = load_table_words(tab3_words[0], "tab3_sb", "A")
        load_scale_rows(tab3_plane, 4, tab3_scales)
        w3_raw = keep.tile([P, H], I32, align_bytes=64)
        nc.sync.dma_start(w3_raw[:], w3_words[0].rearrange("p c i -> p (c i)").bitcast(I32))
        tab_sb = [load_table_words(tab_words[0], "tab_sb0", "E")]
        load_scale_rows(w3_plane, 8, w3_scales)
        offs_sb = load_list(offs, "offs_sb")
        w1_raw[1, 0] = [load_rows(w1[PASS : 2 * PASS, 0:PASS], "w1_raw10", "D")]
        tab_sb.append(load_table_words(tab_words[1], "tab_sb1", "F"))
        load_scale_rows(tab_plane, 8, tab_scales)
        v2_scales = gather(tab2_plane, offs2_sb, U8, "v2_scales")
        v2_words = gather(tab2_sb, offs2_sb, U32, "v2_words")
        w2_dealt = deal_scales(w2_plane, "w2_dealt")

        w1_raw[0, 1] = [load_rows(w1[0:PASS, PASS : 2 * PASS], "w1_raw01", "B")]
        pos2_sb = load_list(pos2, "pos2_sb")
        b0_sb = keep.tile([P, 2, PACK], F32)
        nc.sync.dma_start(b0_sb[:], b0.rearrange("(b p t) -> p b t", b=2, t=PACK))
        pos1_sb = load_list(pos1, "pos1_sb")
        pos3_sb = load_list(pos3, "pos3_sb")
        w1_codes, w1_scales, w1_bf = {}, {}, {}

        def round_w1(a, b):
            pool, slot = (keep, "w1_bf10") if (a, b) == (1, 0) else (rounded, "bf")
            w1_bf[a, b] = pool.tile([P, PASS * PACK], BF16, name=f"w1_bf{a}{b}", tag=slot, align_bytes=64)
            if (a, b) in ((1, 0), (0, 1)):
                dealt = w1_bf[a, b][:].rearrange("p (t m i) -> p t m i", t=PACK, i=PACK)
                raw = w1_raw[a, b][0][:].rearrange("p i (m t) -> p t m i", t=PACK)
                for t in range(PACK):
                    nc.gpsimd.tensor_scalar(dealt[:, t], raw[:, t], 1.0, 0.0, ALU.mult, ALU.add)
            else:
                nc.scalar.copy(
                    w1_bf[a, b][:].rearrange("p (t m i) -> p m i t", t=PACK, i=PACK),
                    w1_raw[a, b][0][:].rearrange("p i (m t) -> p m i t", t=PACK),
                )

        def quantize_w1(a, b):
            pool, slot = {(1, 0): (keep, "tab_plane"), (0, 1): (loads, "A")}.get((a, b), (keep, f"w1_codes{a}{b}"))
            w1_codes[a, b] = pool.tile([P, PASS], U32, name=f"w1_codes{a}{b}", tag=slot, align_bytes=64)
            w1_scales[a, b] = keep.tile([P, PASS], U8, name=f"w1_scales{a}{b}", align_bytes=64)
            nc.vector.quantize_mx(out=w1_codes[a, b][:].bitcast(FP8X4), scales=w1_scales[a, b][:], in_=w1_bf[a, b][:])

        def first_stage(passes, name, halves=(0, 1), window=None):
            if window is None:
                pool, slot = (keep, "a7") if name == "a7" else (windows, "window")
                window = pool.tile([P, S], F32, name=name, tag=slot, align_bytes=64)
            for h in halves:
                cols = slice(h * BANK, (h + 1) * BANK)
                acc = psum.tile([P, BANK], F32, name="acc", tag="bank")
                for n, (lhsT, lhsT_scale, words, scales) in enumerate(passes):
                    nc.tensor.matmul_mx(
                        out=acc[:], lhsT=lhsT, lhsT_scale=lhsT_scale,
                        rhs=words[:, cols].bitcast(FP8X4), rhs_scale=scales[:, cols],
                        start=(n == 0), stop=(n == len(passes) - 1),
                    )
                nc.scalar.copy(window[:, cols], acc[:])
            return window

        round_w1(0, 0)
        w1_raw[1, 1] = [load_rows(w1[PASS : 2 * PASS, PASS : 2 * PASS], "w1_raw11", "C")]
        b_win = {}
        for h, s in [(0, s) for s in range(HF)] + [(1, s) for s in range(HF)] + [(h, s) for s in range(HF, 8) for h in range(2)]:
            cols = slice(s * P, (s + 1) * P)
            lhsT = w2_sb[:, 2 * s * P : 2 * (s + 1) * P].bitcast(FP4X4)
            b_win[s] = first_stage([(lhsT, w2_dealt[:, cols], v2_words, v2_scales)], f"b{s}", (h,), b_win.get(s))
            if (s, h) == (4, 1):
                round_w1(1, 0)

        v3_words = gather(tab3_sb, offs3_sb, U32, "v3_words")
        quantize_w1(0, 0)
        v3_scales = gather(tab3_plane, offs3_sb, U8, "v3_scales")
        w3_sb = keep.tile([P, H], I32, align_bytes=64)
        nc.vector.tensor_copy(
            w3_sb[:].rearrange("p (b t m) -> p b m t", b=2, t=PACK),
            w3_raw[:].rearrange("p (b m t) -> p b m t", b=2, t=PACK),
        )
        w3_dealt = deal_scales(w3_plane, "w3_dealt")
        v_words = [gather(tab_sb[a], offs_sb, U32, f"v_words{a}") for a in range(2)]
        v_scales = gather(tab_plane, offs_sb, U8, "v_scales")
        quantize_w1(1, 0)
        b_picks = keep.tile([P, RING, PICKS], F32, tag="w1_bf10", align_bytes=64)
        w4_raw = [load_rows(w4[a * PASS : (a + 1) * PASS, :], f"w4_raw{a}", "AD"[a]) for a in range(2)]
        w5_sb = keep.tile([P, 2, 2 * N], U8, align_bytes=64)
        nc.sync.dma_start(w5_sb[:].bitcast(I32), w5_words.rearrange("a p c -> p a c").bitcast(I32))
        for q in range(4):
            nc.sync.dma_start(
                w5_plane[32 * q : 32 * q + 4, :].bitcast(I32).rearrange("r (a n) -> r a n", a=2),
                w5_scales[:, 4 * q : 4 * q + 4, :].bitcast(I32).rearrange("a r n -> r a n"),
            )

        w4_codes = keep.tile([P, 2 * N], U32, align_bytes=64)
        w4_scales = keep.tile([P, 2 * N], U8, align_bytes=64)
        w4_bf = keep.tile([P, 2 * N * PACK], BF16, align_bytes=64)
        z_codes, z_scales = [], []

        def gain_of(s):
            b_pick = b_picks[:, s % RING, :]
            nc.vector.tensor_copy(b_pick, b_win[s][:].indirect(pos2_sb[:]))
            gain = gains.tile([P, PICKS], F32, name="gain")
            nc.scalar.activation(gain[:], b_pick, ACT.Tanh, bias=b0_sb[:, s // PACK, s % PACK : s % PACK + 1])
            nc.scalar.activation(gain[:], gain[:], ACT.Exp)
            return gain

        def d_of(s):
            cols = slice(s * P, (s + 1) * P)
            return first_stage([(w3_sb[:, cols].bitcast(FP8X4), w3_dealt[8:P, cols], v3_words, v3_scales[4:P, :])], f"d{s}")

        def a_of(s):
            b, cols = s // PACK, slice(s % PACK * P, (s % PACK + 1) * P)
            return first_stage(
                [(w1_codes[a, b][:, cols].bitcast(FP8X4), w1_scales[a, b][:, cols], v_words[a], v_scales[8 + 4 * a : P, :])
                 for a in range(2)], f"a{s}")

        def round_w4(a, copy):
            copy(
                w4_bf[:, a * N * PACK : (a + 1) * N * PACK].rearrange("p (c e i) -> p c i e", e=4, i=PACK),
                w4_raw[a][:].rearrange("p i (c e) -> p c i e", e=4),
            )

        z_f32 = []

        z_bf = []

        def round_z(b, lo, hi, copy):
            if lo == 0:
                z_bf.append(rounded.tile([P, PICKS * PACK], BF16, name="z_bf", tag="bf", align_bytes=64))
            copy(
                z_bf[b][:, PACK * lo : PACK * hi].rearrange("p (c e t) -> p c t e", e=4, t=PACK),
                z_f32[b][:, :, lo:hi].rearrange("p t (c e) -> p c t e", e=4),
            )

        def quantize_z(b):
            z_codes.append(keep.tile([P, PICKS], U32, name=f"z_codes{b}", tag=("a7", "z_codes1")[b], align_bytes=64))
            z_scales.append(keep.tile([P, PICKS], U8, name=f"z_scales{b}", align_bytes=64))
            nc.vector.quantize_mx(out=z_codes[b][:].bitcast(FP8X4), scales=z_scales[b][:], in_=z_bf[b][:])

        def scale_a(s, a_win, gain):
            scaled = picks.tile([P, PICKS], F32, name="scaled")
            nc.vector.tensor_tensor(scaled[:], a_win[:].indirect(pos1_sb[:]), gain[:], ALU.mult)
            return scaled

        def shift_by_d(s, d_win, scaled, lo, hi):
            b, t = divmod(s, PACK)
            if t == 0 and lo == 0:
                z_f32.append(joined.tile([P, PACK, PICKS], F32, name="z_f32"))
            nc.vector.tensor_tensor(
                z_f32[b][:, t, lo:hi], d_win[:].indirect(pos3_sb[:, lo // 16 : hi // 16]), scaled[:, lo:hi], ALU.add)

        round_w1(0, 1)
        d_win = {s: d_of(s) for s in range(3)}
        round_w1(1, 1)
        quantize_w1(1, 1)
        scaled = {}
        for s in range(8):
            a_win = a_of(s)
            scaled[s] = scale_a(s, a_win, gain_of(s))
            if s > 0:
                if s - 1 not in d_win:
                    d_win[s - 1] = d_of(s - 1)
                shift_by_d(s - 1, d_win[s - 1], scaled[s - 1], 0, PICKS)
            if s == 0:
                round_w4(0, nc.scalar.copy)
                quantize_w1(0, 1)
            if s == 2:
                round_w4(1, nc.scalar.copy)
            if s == 4:
                for lo, hi in ((0, 512), (512, 768)):
                    nc.vector.quantize_mx(
                        out=w4_codes[:, lo:hi].bitcast(FP8X4), scales=w4_scales[:, lo:hi],
                        in_=w4_bf[:, PACK * lo : PACK * hi])
            if s == 5:
                round_z(0, 0, PICKS, nc.vector.tensor_copy)
            if s == 7:
                quantize_z(0)
        last = d_of(7)
        shift_by_d(7, last, scaled[7], 0, PICKS // 2)
        round_z(1, 0, PICKS // 2, nc.scalar.copy)
        shift_by_d(7, last, scaled[7], PICKS // 2, PICKS)
        round_z(1, PICKS // 2, PICKS, nc.vector.tensor_copy)
        quantize_z(1)

        y1 = [psum.tile([P, PICKS], F32, name=f"y1_{n}", tag="bank") for n in range(N // P)]
        y2 = [psum.tile([P, PICKS], F32, name=f"y2_{n}", tag="bank") for n in range(N // P)]
        for a in range(2):
            for n in range(N // P):
                cols = slice(a * N + n * P, a * N + (n + 1) * P)
                nc.tensor.matmul_mx(
                    out=y2[n][:], lhsT=w5_sb[:, a, 2 * n * P : 2 * (n + 1) * P].bitcast(FP4X4),
                    lhsT_scale=w5_plane[:, cols], rhs=z_codes[a][:].bitcast(FP8X4), rhs_scale=z_scales[a][:],
                    start=(a == 0), stop=(a == 1))
                nc.tensor.matmul_mx(
                    out=y1[n][:], lhsT=w4_codes[:, cols].bitcast(FP8X4), lhsT_scale=w4_scales[:, cols],
                    rhs=z_codes[a][:].bitcast(FP8X4), rhs_scale=z_scales[a][:],
                    start=(a == 0), stop=(a == 1))
        for n in range(N // P):
            squared = picks.tile([P, PICKS], F32, name="b_pick", bufs=3)
            result = picks.tile([P, PICKS], F32, name="scaled")
            for lo in range(0, PICKS, PIECE):
                cols = slice(lo, lo + PIECE)
                nc.scalar.activation(squared[:, cols], y2[n][:, cols], ACT.Square)
                nc.vector.tensor_tensor(result[:, cols], y1[n][:, cols], squared[:, cols], ALU.subtract)
                nc.sync.dma_start(out[n * P : (n + 1) * P, cols], result[:, cols])
